import numpy as np
import ml_dtypes


def mxq(x, axis, fmt="e4m3"):
    dtype, down = {"e4m3": (ml_dtypes.float8_e4m3fn, 7), "e5m2": (ml_dtypes.float8_e5m2, 14)}[fmt]
    v = np.moveaxis(np.asarray(x, np.float32).astype(ml_dtypes.bfloat16).astype(np.float64), axis, -1)
    blocks = v.reshape(v.shape[:-1] + (-1, 32))
    amax = np.abs(blocks).max(-1, keepdims=True)
    byte = np.maximum(np.where(amax > 0, np.frexp(amax)[1] - 1 + 127, 0) - down, 1)
    scale = np.exp2(byte - 127.0)
    codes = (blocks / scale).astype(np.float32).astype(dtype).astype(np.float64)
    return np.moveaxis((codes * scale).reshape(v.shape), -1, axis)


WIDE = False


def mx_kscale(k):
    if not WIDE:
        return np.ones(k)
    levels = np.array([30, -30])
    if k % 512:
        return np.exp2(np.random.permutation(np.resize(levels, k // 32))).repeat(32)
    a = np.empty((k // 512, 16))
    for p in range(k // 512):
        a[p, :8] = np.random.permutation(np.resize(levels, 8))
        for g in range(8):
            far = levels[np.abs(levels - a[p, g]) >= 10]
            a[p, g + 8] = far[np.random.randint(len(far))]
    return np.exp2(a.ravel()).repeat(32)


def f64(x):
    return np.asarray(x).astype(np.float64)


def striped(idx):
    return np.tile(np.asarray(idx).reshape(-1, 16).T, (8, 1)).astype(np.uint16)


def unstriped(offs):
    return offs[:16].T.reshape(-1).astype(np.int64)


E2M1 = np.array([0.0, 0.5, 1.0, 1.5, 2.0, 3.0, 4.0, 6.0, -0.0, -0.5, -1.0, -1.5, -2.0, -3.0, -4.0, -6.0])


def pack_weight(w, fmt):
    k, n = w.shape
    w = f64(np.asarray(w, np.float32).astype(ml_dtypes.bfloat16)).reshape(k // 32, 32, n)
    amax = np.abs(w).max(1)
    if fmt in ("e4m3", "e5m2"):
        byte = np.frexp(amax)[1] - 1 + 127 - (7 if fmt == "e4m3" else 14)
    else:
        mant, ex = np.frexp(amax / 6.0)
        byte = np.where(mant > 0.5, ex, ex - 1) + 127
    byte = np.clip(np.where(amax > 0, byte, 1), 1, 254)
    scaled = (w * np.exp2(127.0 - byte)[:, None, :]).reshape(k, n).astype(np.float32)
    by_word = np.ascontiguousarray(scaled.reshape(k // 512, 128, 4, n).transpose(0, 1, 3, 2))
    if fmt in ("e4m3", "e5m2"):
        words = by_word.astype(ml_dtypes.float8_e4m3fn if fmt == "e4m3" else ml_dtypes.float8_e5m2).view(np.uint8)
    else:
        c = by_word.astype(ml_dtypes.float4_e2m1fn).view(np.uint8) & 0xF
        words = (c[..., 0::2] | (c[..., 1::2] << 4)).reshape(k // 512, 128, 2 * n)
    return np.ascontiguousarray(words), np.ascontiguousarray(byte.astype(np.uint8).reshape(k // 512, 16, n))


def unpack_weight(words, scales, fmt):
    g, _, n = scales.shape
    words = np.ascontiguousarray(words).reshape(g, 128, n, -1)
    if fmt in ("e4m3", "e5m2"):
        vals = words.view(ml_dtypes.float8_e4m3fn if fmt == "e4m3" else ml_dtypes.float8_e5m2).astype(np.float64)
    else:
        nib = np.empty((g, 128, n, 4), np.uint8)
        nib[..., 0::2] = words & 0xF
        nib[..., 1::2] = words >> 4
        vals = E2M1[nib]
    vals = vals * np.repeat(np.exp2(scales.astype(np.float64) - 127.0), 8, axis=1)[..., None]
    return vals.transpose(0, 1, 3, 2).reshape(g * 512, n)


K, T, Z, J, R, N = 512, 1024, 1024, 256, 512, 256


def setup_inputs():
    n = np.random.standard_normal
    idx = np.random.permutation(T)[:J]
    idx2 = np.random.permutation(Z)[:J]
    idx3 = np.random.permutation(J)[:J]
    idx4 = np.random.permutation(T)[:J]
    fk = mx_kscale(K)
    fr = mx_kscale(R)
    xtp = pack_weight(n((K, T)) / fk[:, None], "e2m1")
    xop = pack_weight(n((K, Z)) / fk[:, None], "e4m3")
    wp = pack_weight(n((K, R)) * 1 / np.sqrt(K) * fk[:, None] * fr, "e4m3")
    w2p = pack_weight(n((K, R)) * 1 / np.sqrt(K) * fk[:, None] * fr, "e5m2")
    wbp = pack_weight(n((R, N)) * 1 / np.sqrt(R) / fr[:, None], "e2m1")
    wsp = pack_weight(n((K, N)) * 1 / np.sqrt(K) * fk[:, None], "e4m3")
    return {
        "xt_words": xtp[0],
        "xt_scales": xtp[1],
        "xo_words": xop[0],
        "xo_scales": xop[1],
        "w_words": wp[0],
        "w_scales": wp[1],
        "w2_words": w2p[0],
        "w2_scales": w2p[1],
        "sa": (np.random.uniform(0.5, 1.6, (R, 1))).astype(np.float32),
        "wb_words": wbp[0],
        "wb_scales": wbp[1],
        "ws_words": wsp[0],
        "ws_scales": wsp[1],
        "offs": striped(idx),
        "offs2": striped(idx2),
        "offs3": striped(idx3),
        "offs4": striped(idx4),
    }


def reference(xt_words, xt_scales, xo_words, xo_scales, w_words, w_scales, w2_words, w2_scales, sa, wb_words, wb_scales, ws_words, ws_scales, offs, offs2, offs3, offs4):
    idx = unstriped(offs)
    idx2 = unstriped(offs2)
    idx3 = unstriped(offs3)
    idx4 = unstriped(offs4)
    xtu = unpack_weight(xt_words, xt_scales, "e2m1")
    xou = unpack_weight(xo_words, xo_scales, "e4m3")
    wu = unpack_weight(w_words, w_scales, "e4m3")
    w2u = unpack_weight(w2_words, w2_scales, "e5m2")
    wbu = unpack_weight(wb_words, wb_scales, "e2m1")
    wsu = unpack_weight(ws_words, ws_scales, "e4m3")
    xtidxg = xtu[:, idx]
    xoidx2g = xou[:, idx2]
    a = wu.T @ xtidxg + w2u.T @ xoidx2g
    b = w2u.T @ xtidxg + wu.T @ xoidx2g
    hid = np.maximum(a, b[:, idx3] * f64(sa))
    hidq = mxq(hid, 0, "e5m2")
    xtidx4g = xtu[:, idx4]
    y = wbu.T @ hidq + wsu.T @ xtidx4g
    return y

@@ -1,0 +1,185 @@
+from contextlib import ExitStack
+
+import concourse.mybir as mybir
+
+K, T, Z, J, R, N = 512, 1024, 1024, 256, 512, 256
+FLOPS = 2 * K * R * J * 4 + 2 * R * N * J + 2 * K * N * J
+
+F32 = mybir.dt.float32
+BF16 = mybir.dt.bfloat16
+I32 = mybir.dt.int32
+U32 = mybir.dt.uint32
+U16 = mybir.dt.uint16
+U8 = mybir.dt.uint8
+E4M3 = mybir.dt.float8_e4m3fn_x4
+E5M2 = mybir.dt.float8_e5m2_x4
+E2M1 = mybir.dt.float4_e2m1fn_x4
+COPY = mybir.ActivationFunctionType.Copy
+MAX = mybir.AluOpType.max
+
+P = 128
+PACK = 4
+HALF = J // 2
+LIST_COLS = J // 16
+
+
+def load_scale_pairs(queue, staged, scales, cols):
+    rows = scales[0].rearrange("(a b r) n -> b r a n", a=2, b=2)
+    for b in range(2):
+        queue.dma_start(out=staged[32 * b : 32 * b + 4, :, cols].bitcast(I32), in_=rows[b].bitcast(I32))
+
+
+def load_scale_plane(queue, plane, scales):
+    for q in range(4):
+        queue.dma_start(out=plane[32 * q : 32 * q + 4, :].bitcast(I32), in_=scales[0, 4 * q : 4 * q + 4, :].bitcast(I32))
+
+
+def lift_upper_half(nc, staged):
+    nc.vector.tensor_copy(out=staged[64:128, 0, :].bitcast(I32), in_=staged[0:64, 1, :].bitcast(I32))
+
+
+def tile_list_scaledpartner_crossed_further_plain_kernel(
+    tc, xt_words, xt_scales, xo_words, xo_scales, w_words, w_scales, w2_words, w2_scales, sa,
+    wb_words, wb_scales, ws_words, ws_scales, offs, offs2, offs3, offs4, out,
+):
+    nc = tc.nc
+    with ExitStack() as ctx:
+        lists = ctx.enter_context(tc.tile_pool(name="lists", bufs=1))
+        sb = ctx.enter_context(tc.tile_pool(name="sb", bufs=1))
+        psum = ctx.enter_context(tc.psum_pool(name="psum", bufs=1))
+
+        idx1 = lists.tile([P, LIST_COLS], U16, name="idx1")
+        idx2 = lists.tile([P, LIST_COLS], U16, name="idx2")
+        idx3 = lists.tile([P, LIST_COLS], U16, name="idx3")
+        idx4 = lists.tile([P, LIST_COLS], U16, name="idx4")
+
+        xt_w = sb.tile([P, T], U16, name="xt_w", align_bytes=64)
+        xo_w = sb.tile([P, Z], U32, name="xo_w", align_bytes=64)
+        xt_s = sb.tile([P, T], U8, name="xt_s", align_bytes=64)
+        xo_s = sb.tile([P, Z], U8, name="xo_s", align_bytes=64)
+        ww_s = sb.tile([P, 2, 2 * R], U8, name="ww_s", align_bytes=64)
+        w2_raw = sb.tile([P, R], U32, name="w2_raw", tag="raw_a", align_bytes=64)
+        w_raw = sb.tile([P, R], U32, name="w_raw", tag="raw_b", align_bytes=64)
+        sa_t = sb.tile([P, PACK], F32, name="sa_t")
+
+        nc.vector.memset(xt_s[:].bitcast(I32), 0)
+        nc.vector.memset(ww_s[0:64].rearrange("p a n -> p (a n)").bitcast(I32), 0)
+        nc.vector.memset(xo_s[:].bitcast(I32), 0)
+
+        def words32(dram):
+            return dram[0].rearrange("p n t -> p (n t)").bitcast(I32)
+
+        nc.sync.dma_start(idx1[:], offs)
+        nc.sync.dma_start(out=xt_w[:].bitcast(I32), in_=xt_words[0].bitcast(I32))
+        load_scale_plane(nc.scalar, xt_s, xt_scales)
+        nc.sync.dma_start(out=w2_raw[:].bitcast(I32), in_=words32(w2_words))
+        load_scale_pairs(nc.scalar, ww_s, w2_scales, slice(0, R))
+        nc.sync.dma_start(out=w_raw[:].bitcast(I32), in_=words32(w_words))
+        load_scale_pairs(nc.scalar, ww_s, w_scales, slice(R, 2 * R))
+        nc.sync.dma_start(idx2[:], offs2)
+        nc.sync.dma_start(out=xo_w[:].bitcast(I32), in_=words32(xo_words))
+        load_scale_plane(nc.sync, xo_s, xo_scales)
+        nc.sync.dma_start(idx3[:], offs3)
+        nc.sync.dma_start(out=sa_t[:], in_=sa.rearrange("(p t) o -> p (t o)", t=PACK))
+        nc.sync.dma_start(idx4[:], offs4)
+
+        def gather(name, window, idx, dtype):
+            picked = sb.tile([P, J], dtype, name=name, align_bytes=64)
+            nc.vector.tensor_copy(picked[:], window.indirect(idx[:]))
+            return picked
+
+        x1_s = gather("x1_s", xt_s[:], idx1, U8)
+        x1_w = gather("x1_w", xt_w[:], idx1, U16)
+
+        w2_d = sb.tile([P, R], U32, name="w2_d", align_bytes=64)
+        w_d = sb.tile([P, R], U32, name="w_d", align_bytes=64)
+        w2_ds = sb.tile([P, R], U8, name="w2_ds", align_bytes=64)
+        w_ds = sb.tile([P, R], U8, name="w_ds", align_bytes=64)
+        lift_upper_half(nc, ww_s)
+        for dealt, dealt_s, raw, col0 in ((w2_d, w2_ds, w2_raw, 0), (w_d, w_ds, w_raw, R)):
+            nc.scalar.copy(
+                out=dealt[:].rearrange("p (t mh ml) -> p mh t ml", t=PACK, ml=4),
+                in_=raw[:].rearrange("p (mh ml t) -> p mh t ml", t=PACK, ml=4),
+            )
+            nc.vector.tensor_copy(
+                out=dealt_s[:].rearrange("p (t m) -> p t m", t=PACK),
+                in_=ww_s[:, 0, col0 : col0 + R].rearrange("p (m t) -> p t m", t=PACK),
+            )
+
+        x2_s = gather("x2_s", xo_s[:], idx2, U8)
+        x2_w = gather("x2_w", xo_w[:], idx2, U32)
+
+        ws_w = sb.tile([P, N], U32, name="ws_w", tag="raw_a", align_bytes=64)
+        wb_w = sb.tile([P, N], U16, name="wb_w", tag="raw_b", align_bytes=64)
+        nc.sync.dma_start(out=ws_w[:].bitcast(I32), in_=words32(ws_words))
+        nc.sync.dma_start(out=wb_w[:].bitcast(I32), in_=wb_words[0].bitcast(I32))
+        ws_s = ww_s[:, 0, 0:N]
+        wb_s = ww_s[:, 0, N : 2 * N]
+        load_scale_plane(nc.sync, ws_s, ws_scales)
+        load_scale_plane(nc.sync, wb_s, wb_scales)
+
+        def mm(acc, lhs, rhs, lcols, rcols, start, stop):
+            nc.tensor.matmul_mx(
+                out=acc,
+                lhsT=lhs[0][:, lcols].bitcast(lhs[2]), lhsT_scale=lhs[1][:, lcols],
+                rhs=rhs[0][:, rcols].bitcast(rhs[2]), rhs_scale=rhs[1][:, rcols],
+                start=start, stop=stop,
+            )
+
+        op_w, op_w2 = (w_d, w_ds, E4M3), (w2_d, w2_ds, E5M2)
+        op_x1, op_x2 = (x1_w, x1_s, E2M1), (x2_w, x2_s, E4M3)
+        rows = [slice(P * t, P * (t + 1)) for t in range(PACK)]
+        halves = [slice(HALF * h, HALF * (h + 1)) for h in range(2)]
+        every = slice(0, J)
+
+        b_ps = [psum.tile([P, J], F32, name=f"b_ps{t}") for t in range(PACK)]
+        a_ps = [psum.tile([P, PACK, HALF], F32, name=f"a_ps{h}") for h in range(2)]
+        y_ps = [psum.tile([P, 2, HALF], F32, name=f"y_ps{h}") for h in range(2)]
+
+        for t in range(PACK):
+            mm(b_ps[t][:], op_w2, op_x1, rows[t], every, True, False)
+        b_sb = []
+        for t in range(PACK):
+            mm(b_ps[t][:], op_w, op_x2, rows[t], every, False, True)
+            b_t = sb.tile([P, J], F32, name=f"b_sb{t}", align_bytes=64)
+            nc.vector.tensor_copy(b_t[:], b_ps[t][:])
+            b_sb.append(b_t)
+        for h in range(2):
+            for t in range(PACK):
+                mm(a_ps[h][:, t, :], op_w, op_x1, rows[t], halves[h], t == 0, False)
+        for h in range(2):
+            for t in range(PACK):
+                mm(a_ps[h][:, t, :], op_w2, op_x2, rows[t], halves[h], False, t == PACK - 1)
+
+        x4_s = gather("x4_s", xt_s[:], idx4, U8)
+        x4_w = gather("x4_w", xt_w[:], idx4, U16)
+        op_x4 = (x4_w, x4_s, E2M1)
+        op_ws, op_wb = (ws_w, ws_s, E4M3), (wb_w, wb_s, E2M1)
+        for h in range(2):
+            for nt in range(2):
+                mm(y_ps[h][:, nt, :], op_ws, op_x4, rows[nt], halves[h], nt == 0, False)
+
+        partner = [sb.tile([P, PACK, HALF], F32, name=f"partner{h}", align_bytes=64) for h in range(2)]
+        for h in range(2):
+            list_cols = slice(h * LIST_COLS // 2, (h + 1) * LIST_COLS // 2)
+            for t in range(PACK):
+                nc.scalar.activation(
+                    out=partner[h][:, t, :], in_=b_sb[t][:].indirect(idx3[:, list_cols]), func=COPY,
+                    scale=sa_t[:, t : t + 1],
+                )
+
+        out_v = out.rearrange("(nt p) j -> p nt j", p=P)
+        for h in range(2):
+            hid = sb.tile([P, HALF, PACK], BF16, name=f"hid{h}", align_bytes=64)
+            nc.vector.tensor_tensor(
+                out=hid[:], in0=a_ps[h][:].rearrange("p t j -> p j t"),
+                in1=partner[h][:].rearrange("p t j -> p j t"), op=MAX,
+            )
+            hq_w = sb.tile([P, HALF], U32, name=f"hq_w{h}", align_bytes=64)
+            hq_s = sb.tile([P, HALF], U8, name=f"hq_s{h}", align_bytes=64)
+            nc.vector.quantize_mx(out=hq_w[:].bitcast(E5M2), scales=hq_s[:], in_=hid[:].rearrange("p j t -> p (j t)"))
+            for nt in range(2):
+                mm(y_ps[h][:, nt, :], op_wb, (hq_w, hq_s, E5M2), rows[nt], slice(0, HALF), False, nt == 1)
+            y_sb = sb.tile([P, 2, HALF], F32, name=f"y_sb{h}", align_bytes=64)
+            nc.scalar.copy(out=y_sb[:], in_=y_ps[h][:])
+            nc.sync.dma_start(out=out_v[:, :, halves[h]], in_=y_sb[:])

@@ -29,8 +29,8 @@ def load_scale_pairs(queue, staged, scales, cols):
         queue.dma_start(out=staged[32 * b : 32 * b + 4, :, cols].bitcast(I32), in_=rows[b].bitcast(I32))
 
 
-def load_scale_plane(queue, plane, scales):
-    for q in range(4):
+def load_scale_plane(queue, plane, scales, quadrants=range(4)):
+    for q in quadrants:
         queue.dma_start(out=plane[32 * q : 32 * q + 4, :].bitcast(I32), in_=scales[0, 4 * q : 4 * q + 4, :].bitcast(I32))
 
 
@@ -46,6 +46,7 @@ def tile_list_scaledpartner_crossed_further_plain_kernel(
     with ExitStack() as ctx:
         lists = ctx.enter_context(tc.tile_pool(name="lists", bufs=1))
         sb = ctx.enter_context(tc.tile_pool(name="sb", bufs=1))
+        reuse = ctx.enter_context(tc.tile_pool(name="reuse", bufs=1))
         psum = ctx.enter_context(tc.psum_pool(name="psum", bufs=1))
 
         idx1 = lists.tile([P, LIST_COLS], U16, name="idx1")
@@ -58,38 +59,47 @@ def tile_list_scaledpartner_crossed_further_plain_kernel(
         xt_s = sb.tile([P, T], U8, name="xt_s", align_bytes=64)
         xo_s = sb.tile([P, Z], U8, name="xo_s", align_bytes=64)
         ww_s = sb.tile([P, 2, 2 * R], U8, name="ww_s", align_bytes=64)
-        w2_raw = sb.tile([P, R], U32, name="w2_raw", tag="raw_a", align_bytes=64)
-        w_raw = sb.tile([P, R], U32, name="w_raw", tag="raw_b", align_bytes=64)
+        w2_raw = reuse.tile([P, R], U32, name="w2_raw", offset=0, align_bytes=64)
+        w_raw = reuse.tile([P, R], U32, name="w_raw", offset=4 * R, align_bytes=64)
         sa_t = sb.tile([P, PACK], F32, name="sa_t")
 
         nc.vector.memset(xt_s[:].bitcast(I32), 0)
         nc.vector.memset(ww_s[0:64].rearrange("p a n -> p (a n)").bitcast(I32), 0)
-        nc.vector.memset(xo_s[:].bitcast(I32), 0)
+        nc.gpsimd.memset(xo_s[:].bitcast(I32), 0)
+        b_sb = [
+            sb.tile([P, J if t == PACK - 1 else 2 * J], F32, name=f"b_sb{t}", align_bytes=64) for t in range(PACK)
+        ]
+        for t in range(PACK - 1):
+            nc.vector.memset(b_sb[t][:, J:], 0.0)
 
         def words32(dram):
             return dram[0].rearrange("p n t -> p (n t)").bitcast(I32)
 
+        load_scale_plane(nc.gpsimd, xo_s, xo_scales, (2, 3))
         nc.sync.dma_start(idx1[:], offs)
         nc.sync.dma_start(out=xt_w[:].bitcast(I32), in_=xt_words[0].bitcast(I32))
-        load_scale_plane(nc.scalar, xt_s, xt_scales)
-        nc.sync.dma_start(out=w2_raw[:].bitcast(I32), in_=words32(w2_words))
-        load_scale_pairs(nc.scalar, ww_s, w2_scales, slice(0, R))
-        nc.sync.dma_start(out=w_raw[:].bitcast(I32), in_=words32(w_words))
-        load_scale_pairs(nc.scalar, ww_s, w_scales, slice(R, 2 * R))
+        load_scale_plane(nc.sync, xt_s, xt_scales)
         nc.sync.dma_start(idx2[:], offs2)
         nc.sync.dma_start(out=xo_w[:].bitcast(I32), in_=words32(xo_words))
-        load_scale_plane(nc.sync, xo_s, xo_scales)
+        nc.sync.dma_start(out=w2_raw[:].bitcast(I32), in_=words32(w2_words))
+        load_scale_pairs(nc.sync, ww_s, w2_scales, slice(0, R))
+        load_scale_pairs(nc.sync, ww_s, w_scales, slice(R, 2 * R))
+        nc.sync.dma_start(out=w_raw[:].bitcast(I32), in_=words32(w_words))
+        load_scale_plane(nc.sync, xo_s, xo_scales, (0, 1))
+        nc.sync.dma_start(idx4[:], offs4)
         nc.sync.dma_start(idx3[:], offs3)
         nc.sync.dma_start(out=sa_t[:], in_=sa.rearrange("(p t) o -> p (t o)", t=PACK))
-        nc.sync.dma_start(idx4[:], offs4)
 
-        def gather(name, window, idx, dtype):
-            picked = sb.tile([P, J], dtype, name=name, align_bytes=64)
-            nc.vector.tensor_copy(picked[:], window.indirect(idx[:]))
-            return picked
+        def gather(picked, window, idx):
+            nc.vector.tensor_copy(picked[:], window[:].indirect(idx[:]))
 
-        x1_s = gather("x1_s", xt_s[:], idx1, U8)
-        x1_w = gather("x1_w", xt_w[:], idx1, U16)
+        x1_w = sb.tile([P, J], U16, name="x1_w", align_bytes=64)
+        x1_s = sb.tile([P, J], U8, name="x1_s", align_bytes=64)
+        x2_w = sb.tile([P, J], U32, name="x2_w", align_bytes=64)
+        x2_s = sb.tile([P, J], U8, name="x2_s", align_bytes=64)
+        gather(x1_w, xt_w, idx1)
+        gather(x1_s, xt_s, idx1)
+        gather(x2_w, xo_w, idx2)
 
         w2_d = sb.tile([P, R], U32, name="w2_d", align_bytes=64)
         w_d = sb.tile([P, R], U32, name="w_d", align_bytes=64)
@@ -98,19 +108,23 @@ def tile_list_scaledpartner_crossed_further_plain_kernel(
         lift_upper_half(nc, ww_s)
         for dealt, dealt_s, raw, col0 in ((w2_d, w2_ds, w2_raw, 0), (w_d, w_ds, w_raw, R)):
             nc.scalar.copy(
-                out=dealt[:].rearrange("p (t mh ml) -> p mh t ml", t=PACK, ml=4),
-                in_=raw[:].rearrange("p (mh ml t) -> p mh t ml", t=PACK, ml=4),
+                out=dealt[:].rearrange("p (t m) -> p m t", t=PACK),
+                in_=raw[:].rearrange("p (m t) -> p m t", t=PACK),
             )
             nc.vector.tensor_copy(
                 out=dealt_s[:].rearrange("p (t m) -> p t m", t=PACK),
                 in_=ww_s[:, 0, col0 : col0 + R].rearrange("p (m t) -> p t m", t=PACK),
             )
 
-        x2_s = gather("x2_s", xo_s[:], idx2, U8)
-        x2_w = gather("x2_w", xo_w[:], idx2, U32)
+        gather(x2_s, xo_s, idx2)
 
-        ws_w = sb.tile([P, N], U32, name="ws_w", tag="raw_a", align_bytes=64)
-        wb_w = sb.tile([P, N], U16, name="wb_w", tag="raw_b", align_bytes=64)
+        x4_s = reuse.tile([P, J], U8, name="x4_s", offset=4 * R, align_bytes=64)
+        x4_w = reuse.tile([P, J], U16, name="x4_w", offset=4 * R + J, align_bytes=64)
+        gather(x4_s, xt_s, idx4)
+        gather(x4_w, xt_w, idx4)
+
+        ws_w = reuse.tile([P, N], U32, name="ws_w", offset=0, align_bytes=64)
+        wb_w = reuse.tile([P, N], U16, name="wb_w", offset=4 * N, align_bytes=64)
         nc.sync.dma_start(out=ws_w[:].bitcast(I32), in_=words32(ws_words))
         nc.sync.dma_start(out=wb_w[:].bitcast(I32), in_=wb_words[0].bitcast(I32))
         ws_s = ww_s[:, 0, 0:N]
@@ -132,54 +146,65 @@ def tile_list_scaledpartner_crossed_further_plain_kernel(
         halves = [slice(HALF * h, HALF * (h + 1)) for h in range(2)]
         every = slice(0, J)
 
-        b_ps = [psum.tile([P, J], F32, name=f"b_ps{t}") for t in range(PACK)]
-        a_ps = [psum.tile([P, PACK, HALF], F32, name=f"a_ps{h}") for h in range(2)]
-        y_ps = [psum.tile([P, 2, HALF], F32, name=f"y_ps{h}") for h in range(2)]
+        b_ps = [psum.tile([P, J], F32, name=f"b_ps{t}", tag=f"bank{t}") for t in range(PACK)]
+        a_ps = [psum.tile([P, 2, J], F32, name=f"a_ps{u}") for u in range(2)]
 
-        for t in range(PACK):
+        EARLY = 3
+        for t in range(EARLY):
             mm(b_ps[t][:], op_w2, op_x1, rows[t], every, True, False)
-        b_sb = []
         for t in range(PACK):
-            mm(b_ps[t][:], op_w, op_x2, rows[t], every, False, True)
-            b_t = sb.tile([P, J], F32, name=f"b_sb{t}", align_bytes=64)
-            nc.vector.tensor_copy(b_t[:], b_ps[t][:])
-            b_sb.append(b_t)
-        for h in range(2):
-            for t in range(PACK):
-                mm(a_ps[h][:, t, :], op_w, op_x1, rows[t], halves[h], t == 0, False)
-        for h in range(2):
-            for t in range(PACK):
-                mm(a_ps[h][:, t, :], op_w2, op_x2, rows[t], halves[h], False, t == PACK - 1)
+            mm(b_ps[t][:], op_w, op_x2, rows[t], every, t >= EARLY, t < EARLY)
+            if t >= EARLY:
+                mm(b_ps[t][:], op_w2, op_x1, rows[t], every, False, True)
+            if t == 0:
+                nc.scalar.copy(b_sb[t][:, 0:J], b_ps[t][:])
+            else:
+                nc.vector.tensor_copy(b_sb[t][:, 0:J], b_ps[t][:])
+        for t in range(PACK):
+            mm(a_ps[t // 2][:, t % 2, :], op_w2, op_x2, rows[t], every, True, False)
+            mm(a_ps[t // 2][:, t % 2, :], op_w, op_x1, rows[t], every, False, True)
 
-        x4_s = gather("x4_s", xt_s[:], idx4, U8)
-        x4_w = gather("x4_w", xt_w[:], idx4, U16)
         op_x4 = (x4_w, x4_s, E2M1)
         op_ws, op_wb = (ws_w, ws_s, E4M3), (wb_w, wb_s, E2M1)
+        y_ps = [[psum.tile([P, HALF], F32, name=f"y_ps{h}{nt}", tag=f"bank{2 * h + nt}") for nt in range(2)] for h in range(2)]
         for h in range(2):
             for nt in range(2):
-                mm(y_ps[h][:, nt, :], op_ws, op_x4, rows[nt], halves[h], nt == 0, False)
+                mm(y_ps[h][nt][:], op_ws, op_x4, rows[nt], halves[h], True, False)
 
-        partner = [sb.tile([P, PACK, HALF], F32, name=f"partner{h}", align_bytes=64) for h in range(2)]
-        for h in range(2):
-            list_cols = slice(h * LIST_COLS // 2, (h + 1) * LIST_COLS // 2)
-            for t in range(PACK):
-                nc.scalar.activation(
-                    out=partner[h][:, t, :], in_=b_sb[t][:].indirect(idx3[:, list_cols]), func=COPY,
-                    scale=sa_t[:, t : t + 1],
-                )
+        partner = [sb.tile([P, 2, J], F32, name=f"partner{u}", align_bytes=64) for u in range(2)]
+        hid = [sb.tile([P, HALF, PACK], BF16, name=f"hid{h}", align_bytes=64) for h in range(2)]
 
-        out_v = out.rearrange("(nt p) j -> p nt j", p=P)
-        for h in range(2):
-            hid = sb.tile([P, HALF, PACK], BF16, name=f"hid{h}", align_bytes=64)
-            nc.vector.tensor_tensor(
-                out=hid[:], in0=a_ps[h][:].rearrange("p t j -> p j t"),
-                in1=partner[h][:].rearrange("p t j -> p j t"), op=MAX,
+        def look_up(t, cols):
+            nc.scalar.activation(
+                out=partner[t // 2][:, t % 2, cols],
+                in_=b_sb[t][:].indirect(idx3[:, cols.start // 16 : cols.stop // 16]),
+                func=COPY, scale=sa_t[:, t : t + 1],
             )
+
+        def keep_larger(u, h):
+            nc.vector.tensor_tensor(
+                out=hid[h][:, :, 2 * u : 2 * u + 2].rearrange("p (c i) t -> p c t i", i=4),
+                in0=a_ps[u][:, :, halves[h]].rearrange("p t (c i) -> p c t i", i=4),
+                in1=partner[u][:, :, halves[h]].rearrange("p t (c i) -> p c t i", i=4), op=MAX,
+            )
+
+        for t in range(PACK - 1):
+            look_up(t, every)
+        for h in range(2):
+            look_up(PACK - 1, halves[h])
+        for h in range(2):
+            keep_larger(0, h)
+        for h in range(2):
+            keep_larger(1, h)
             hq_w = sb.tile([P, HALF], U32, name=f"hq_w{h}", align_bytes=64)
             hq_s = sb.tile([P, HALF], U8, name=f"hq_s{h}", align_bytes=64)
-            nc.vector.quantize_mx(out=hq_w[:].bitcast(E5M2), scales=hq_s[:], in_=hid[:].rearrange("p j t -> p (j t)"))
+            nc.vector.quantize_mx(out=hq_w[:].bitcast(E5M2), scales=hq_s[:], in_=hid[h][:].rearrange("p j t -> p (j t)"))
             for nt in range(2):
-                mm(y_ps[h][:, nt, :], op_wb, (hq_w, hq_s, E5M2), rows[nt], slice(0, HALF), False, nt == 1)
-            y_sb = sb.tile([P, 2, HALF], F32, name=f"y_sb{h}", align_bytes=64)
-            nc.scalar.copy(out=y_sb[:], in_=y_ps[h][:])
-            nc.sync.dma_start(out=out_v[:, :, halves[h]], in_=y_sb[:])
+                mm(y_ps[h][nt][:], op_wb, (hq_w, hq_s, E5M2), rows[nt], slice(0, HALF), False, True)
+                y_sb = sb.tile([P, HALF], F32, name=f"y_sb{h}{nt}", align_bytes=64)
+                if h == 1 and nt == 0:
+                    nc.vector.tensor_copy(y_sb[:], y_ps[h][nt][:])
+                else:
+                    nc.scalar.copy(y_sb[:], y_ps[h][nt][:])
+                queue = nc.scalar if (h == 1 and nt == 1) else nc.sync
+                queue.dma_start(out=out[rows[nt], halves[h]], in_=y_sb[:])

from contextlib import ExitStack

import concourse.mybir as mybir

K, T, Z, J, R, N = 512, 1024, 1024, 256, 512, 256
FLOPS = 2 * K * R * J * 4 + 2 * R * N * J + 2 * K * N * J

F32 = mybir.dt.float32
BF16 = mybir.dt.bfloat16
I32 = mybir.dt.int32
U32 = mybir.dt.uint32
U16 = mybir.dt.uint16
U8 = mybir.dt.uint8
E4M3 = mybir.dt.float8_e4m3fn_x4
E5M2 = mybir.dt.float8_e5m2_x4
E2M1 = mybir.dt.float4_e2m1fn_x4
COPY = mybir.ActivationFunctionType.Copy
MAX = mybir.AluOpType.max

P = 128
PACK = 4
HALF = J // 2
LIST_COLS = J // 16


def load_scale_pairs(queue, staged, scales, cols):
    rows = scales[0].rearrange("(a b r) n -> b r a n", a=2, b=2)
    for b in range(2):
        queue.dma_start(out=staged[32 * b : 32 * b + 4, :, cols].bitcast(I32), in_=rows[b].bitcast(I32))


def load_scale_plane(queue, plane, scales, quadrants=range(4)):
    for q in quadrants:
        queue.dma_start(out=plane[32 * q : 32 * q + 4, :].bitcast(I32), in_=scales[0, 4 * q : 4 * q + 4, :].bitcast(I32))


def lift_upper_half(nc, staged):
    nc.vector.tensor_copy(out=staged[64:128, 0, :].bitcast(I32), in_=staged[0:64, 1, :].bitcast(I32))


def tile_list_scaledpartner_crossed_further_plain_kernel(
    tc, xt_words, xt_scales, xo_words, xo_scales, w_words, w_scales, w2_words, w2_scales, sa,
    wb_words, wb_scales, ws_words, ws_scales, offs, offs2, offs3, offs4, out,
):
    nc = tc.nc
    with ExitStack() as ctx:
        lists = ctx.enter_context(tc.tile_pool(name="lists", bufs=1))
        sb = ctx.enter_context(tc.tile_pool(name="sb", bufs=1))
        reuse = ctx.enter_context(tc.tile_pool(name="reuse", bufs=1))
        psum = ctx.enter_context(tc.psum_pool(name="psum", bufs=1))

        idx1 = lists.tile([P, LIST_COLS], U16, name="idx1")
        idx2 = lists.tile([P, LIST_COLS], U16, name="idx2")
        idx3 = lists.tile([P, LIST_COLS], U16, name="idx3")
        idx4 = lists.tile([P, LIST_COLS], U16, name="idx4")

        xt_w = sb.tile([P, T], U16, name="xt_w", align_bytes=64)
        xo_w = sb.tile([P, Z], U32, name="xo_w", align_bytes=64)
        xt_s = sb.tile([P, T], U8, name="xt_s", align_bytes=64)
        xo_s = sb.tile([P, Z], U8, name="xo_s", align_bytes=64)
        ww_s = sb.tile([P, 2, 2 * R], U8, name="ww_s", align_bytes=64)
        w2_raw = reuse.tile([P, R], U32, name="w2_raw", offset=0, align_bytes=64)
        w_raw = reuse.tile([P, R], U32, name="w_raw", offset=4 * R, align_bytes=64)
        sa_t = sb.tile([P, PACK], F32, name="sa_t")

        nc.vector.memset(xt_s[:].bitcast(I32), 0)
        nc.vector.memset(ww_s[0:64].rearrange("p a n -> p (a n)").bitcast(I32), 0)
        nc.gpsimd.memset(xo_s[:].bitcast(I32), 0)
        b_sb = [
            sb.tile([P, J if t == PACK - 1 else 2 * J], F32, name=f"b_sb{t}", align_bytes=64) for t in range(PACK)
        ]
        for t in range(PACK - 1):
            nc.vector.memset(b_sb[t][:, J:], 0.0)

        def words32(dram):
            return dram[0].rearrange("p n t -> p (n t)").bitcast(I32)

        load_scale_plane(nc.gpsimd, xo_s, xo_scales, (2, 3))
        nc.sync.dma_start(idx1[:], offs)
        nc.sync.dma_start(out=xt_w[:].bitcast(I32), in_=xt_words[0].bitcast(I32))
        load_scale_plane(nc.sync, xt_s, xt_scales)
        nc.sync.dma_start(idx2[:], offs2)
        nc.sync.dma_start(out=xo_w[:].bitcast(I32), in_=words32(xo_words))
        nc.sync.dma_start(out=w2_raw[:].bitcast(I32), in_=words32(w2_words))
        load_scale_pairs(nc.sync, ww_s, w2_scales, slice(0, R))
        load_scale_pairs(nc.sync, ww_s, w_scales, slice(R, 2 * R))
        nc.sync.dma_start(out=w_raw[:].bitcast(I32), in_=words32(w_words))
        load_scale_plane(nc.sync, xo_s, xo_scales, (0, 1))
        nc.sync.dma_start(idx4[:], offs4)
        nc.sync.dma_start(idx3[:], offs3)
        nc.sync.dma_start(out=sa_t[:], in_=sa.rearrange("(p t) o -> p (t o)", t=PACK))

        def gather(picked, window, idx):
            nc.vector.tensor_copy(picked[:], window[:].indirect(idx[:]))

        x1_w = sb.tile([P, J], U16, name="x1_w", align_bytes=64)
        x1_s = sb.tile([P, J], U8, name="x1_s", align_bytes=64)
        x2_w = sb.tile([P, J], U32, name="x2_w", align_bytes=64)
        x2_s = sb.tile([P, J], U8, name="x2_s", align_bytes=64)
        gather(x1_w, xt_w, idx1)
        gather(x1_s, xt_s, idx1)
        gather(x2_w, xo_w, idx2)

        w2_d = sb.tile([P, R], U32, name="w2_d", align_bytes=64)
        w_d = sb.tile([P, R], U32, name="w_d", align_bytes=64)
        w2_ds = sb.tile([P, R], U8, name="w2_ds", align_bytes=64)
        w_ds = sb.tile([P, R], U8, name="w_ds", align_bytes=64)
        lift_upper_half(nc, ww_s)
        for dealt, dealt_s, raw, col0 in ((w2_d, w2_ds, w2_raw, 0), (w_d, w_ds, w_raw, R)):
            nc.scalar.copy(
                out=dealt[:].rearrange("p (t m) -> p m t", t=PACK),
                in_=raw[:].rearrange("p (m t) -> p m t", t=PACK),
            )
            nc.vector.tensor_copy(
                out=dealt_s[:].rearrange("p (t m) -> p t m", t=PACK),
                in_=ww_s[:, 0, col0 : col0 + R].rearrange("p (m t) -> p t m", t=PACK),
            )

        gather(x2_s, xo_s, idx2)

        x4_s = reuse.tile([P, J], U8, name="x4_s", offset=4 * R, align_bytes=64)
        x4_w = reuse.tile([P, J], U16, name="x4_w", offset=4 * R + J, align_bytes=64)
        gather(x4_s, xt_s, idx4)
        gather(x4_w, xt_w, idx4)

        ws_w = reuse.tile([P, N], U32, name="ws_w", offset=0, align_bytes=64)
        wb_w = reuse.tile([P, N], U16, name="wb_w", offset=4 * N, align_bytes=64)
        nc.sync.dma_start(out=ws_w[:].bitcast(I32), in_=words32(ws_words))
        nc.sync.dma_start(out=wb_w[:].bitcast(I32), in_=wb_words[0].bitcast(I32))
        ws_s = ww_s[:, 0, 0:N]
        wb_s = ww_s[:, 0, N : 2 * N]
        load_scale_plane(nc.sync, ws_s, ws_scales)
        load_scale_plane(nc.sync, wb_s, wb_scales)

        def mm(acc, lhs, rhs, lcols, rcols, start, stop):
            nc.tensor.matmul_mx(
                out=acc,
                lhsT=lhs[0][:, lcols].bitcast(lhs[2]), lhsT_scale=lhs[1][:, lcols],
                rhs=rhs[0][:, rcols].bitcast(rhs[2]), rhs_scale=rhs[1][:, rcols],
                start=start, stop=stop,
            )

        op_w, op_w2 = (w_d, w_ds, E4M3), (w2_d, w2_ds, E5M2)
        op_x1, op_x2 = (x1_w, x1_s, E2M1), (x2_w, x2_s, E4M3)
        rows = [slice(P * t, P * (t + 1)) for t in range(PACK)]
        halves = [slice(HALF * h, HALF * (h + 1)) for h in range(2)]
        every = slice(0, J)

        b_ps = [psum.tile([P, J], F32, name=f"b_ps{t}", tag=f"bank{t}") for t in range(PACK)]
        a_ps = [psum.tile([P, 2, J], F32, name=f"a_ps{u}") for u in range(2)]

        EARLY = 3
        for t in range(EARLY):
            mm(b_ps[t][:], op_w2, op_x1, rows[t], every, True, False)
        for t in range(PACK):
            mm(b_ps[t][:], op_w, op_x2, rows[t], every, t >= EARLY, t < EARLY)
            if t >= EARLY:
                mm(b_ps[t][:], op_w2, op_x1, rows[t], every, False, True)
            if t == 0:
                nc.scalar.copy(b_sb[t][:, 0:J], b_ps[t][:])
            else:
                nc.vector.tensor_copy(b_sb[t][:, 0:J], b_ps[t][:])
        for t in range(PACK):
            mm(a_ps[t // 2][:, t % 2, :], op_w2, op_x2, rows[t], every, True, False)
            mm(a_ps[t // 2][:, t % 2, :], op_w, op_x1, rows[t], every, False, True)

        op_x4 = (x4_w, x4_s, E2M1)
        op_ws, op_wb = (ws_w, ws_s, E4M3), (wb_w, wb_s, E2M1)
        y_ps = [[psum.tile([P, HALF], F32, name=f"y_ps{h}{nt}", tag=f"bank{2 * h + nt}") for nt in range(2)] for h in range(2)]
        for h in range(2):
            for nt in range(2):
                mm(y_ps[h][nt][:], op_ws, op_x4, rows[nt], halves[h], True, False)

        partner = [sb.tile([P, 2, J], F32, name=f"partner{u}", align_bytes=64) for u in range(2)]
        hid = [sb.tile([P, HALF, PACK], BF16, name=f"hid{h}", align_bytes=64) for h in range(2)]

        def look_up(t, cols):
            nc.scalar.activation(
                out=partner[t // 2][:, t % 2, cols],
                in_=b_sb[t][:].indirect(idx3[:, cols.start // 16 : cols.stop // 16]),
                func=COPY, scale=sa_t[:, t : t + 1],
            )

        def keep_larger(u, h):
            nc.vector.tensor_tensor(
                out=hid[h][:, :, 2 * u : 2 * u + 2].rearrange("p (c i) t -> p c t i", i=4),
                in0=a_ps[u][:, :, halves[h]].rearrange("p t (c i) -> p c t i", i=4),
                in1=partner[u][:, :, halves[h]].rearrange("p t (c i) -> p c t i", i=4), op=MAX,
            )

        for t in range(PACK - 1):
            look_up(t, every)
        for h in range(2):
            look_up(PACK - 1, halves[h])
        for h in range(2):
            keep_larger(0, h)
        for h in range(2):
            keep_larger(1, h)
            hq_w = sb.tile([P, HALF], U32, name=f"hq_w{h}", align_bytes=64)
            hq_s = sb.tile([P, HALF], U8, name=f"hq_s{h}", align_bytes=64)
            nc.vector.quantize_mx(out=hq_w[:].bitcast(E5M2), scales=hq_s[:], in_=hid[h][:].rearrange("p j t -> p (j t)"))
            for nt in range(2):
                mm(y_ps[h][nt][:], op_wb, (hq_w, hq_s, E5M2), rows[nt], slice(0, HALF), False, True)
                y_sb = sb.tile([P, HALF], F32, name=f"y_sb{h}{nt}", align_bytes=64)
                if h == 1 and nt == 0:
                    nc.vector.tensor_copy(y_sb[:], y_ps[h][nt][:])
                else:
                    nc.scalar.copy(y_sb[:], y_ps[h][nt][:])
                queue = nc.scalar if (h == 1 and nt == 1) else nc.sync
                queue.dma_start(out=out[rows[nt], halves[h]], in_=y_sb[:])
